import numpy as np
import ml_dtypes

BF16 = ml_dtypes.bfloat16


def bf(x):
    return np.asarray(x, np.float32).astype(BF16)


def f32(x):
    return np.asarray(x, np.float32)


def f64(x):
    return np.asarray(x).astype(np.float64)


def striped(idx):
    return np.tile(idx.reshape(-1, 16).T, (8, 1))


S, K, M, N, B, Q = 256, 128, 256, 192, 2, 96


def setup_inputs():
    return {"base": bf(np.random.standard_normal((B, M, S))), "x": bf(np.random.standard_normal((K, N))), "w": bf(np.random.standard_normal((K, M)) / np.sqrt(K)), "s": f32(0.5 + np.random.random_sample((M, 1))), "b": f32(0.5 * np.random.standard_normal((M, 1))), "offs": striped(np.random.permutation(S)[:N])}


def reference(base, x, w, s, b, offs):
    idx = offs[:16].T.reshape(-1)
    z = f64(base).copy()
    for i in range(B):
        z[i][:, idx[i * Q : (i + 1) * Q]] += f64(w).T @ f64(x)[:, i * Q : (i + 1) * Q]
    return z * f64(s) + f64(b)

@@ -1,0 +1,64 @@
+import concourse.mybir as mybir
+from concourse.masks import make_identity
+
+BF16, F32, U16 = mybir.dt.bfloat16, mybir.dt.float32, mybir.dt.uint16
+MULT, ADD = mybir.AluOpType.mult, mybir.AluOpType.add
+IDENTITY = mybir.ActivationFunctionType.Identity
+P = 128
+S, K, M, N, B = 256, 128, 256, 192, 2
+PIECE = N // B
+PIECE_COLS = PIECE // 16
+BLOCKS = M // P
+FLOPS = 2 * K * M * N + 2 * B * M * S
+
+
+def tile_scatter_matmul_kernel(tc, base, x, w, s, b, offs, out):
+    nc = tc.nc
+    base_blocks = base.rearrange("i (a p) t -> i p a t", p=P)
+    out_blocks = out.rearrange("i (a p) t -> i a p t", p=P)
+    with (
+        tc.tile_pool(name="held", bufs=1) as held,
+        tc.psum_pool(name="windows", bufs=1) as windows,
+    ):
+        base_tiles = [held.tile([P, BLOCKS, S], BF16, name=f"base{i}") for i in range(B)]
+        offsets = held.tile([P, N // 16], U16, name="offsets")
+        weights = held.tile([P, M], BF16, name="weights")
+        moving = held.tile([P, N], BF16, name="moving")
+        gain = held.tile([P, BLOCKS], F32, name="gain")
+        shift = held.tile([P, BLOCKS], F32, name="shift")
+        for i in range(B):
+            nc.sync.dma_start(base_tiles[i][:], base_blocks[i])
+        nc.sync.dma_start(weights[:], w)
+        nc.sync.dma_start(moving[:], x)
+        nc.sync.dma_start(offsets[:], offs)
+        nc.sync.dma_start(gain[:], s.rearrange("(a p) o -> p (a o)", p=P))
+        nc.sync.dma_start(shift[:], b.rearrange("(a p) o -> p (a o)", p=P))
+
+        ident = held.tile([P, P], BF16, name="ident")
+        make_identity(nc, ident[:])
+
+        places = [(i, a) for i in range(B) for a in range(BLOCKS)]
+        window = {
+            (i, a): windows.tile([P, S], F32, name=f"window{i}{a}") for i, a in places
+        }
+        for i, a in places:
+            nc.tensor.matmul(window[i, a][:], ident[:], base_tiles[i][:, a, :], start=True, stop=False)
+
+        for i, a in places:
+            piece = offsets[:, i * PIECE_COLS : (i + 1) * PIECE_COLS]
+            nc.tensor.matmul(
+                window[i, a][:].indirect(piece),
+                weights[:, a * P : (a + 1) * P],
+                moving[:, i * PIECE : (i + 1) * PIECE],
+                start=False,
+                stop=True,
+            )
+
+        for i, a in places:
+            result = held.tile([P, S], F32, name=f"result{i}{a}")
+            gain_a, shift_a = gain[:, a : a + 1], shift[:, a : a + 1]
+            if a == 0:
+                nc.scalar.activation(result[:], window[i, a][:], IDENTITY, bias=shift_a, scale=gain_a)
+            else:
+                nc.vector.tensor_scalar(result[:], window[i, a][:], gain_a, shift_a, MULT, ADD)
+            nc.sync.dma_start(out_blocks[i, a], result[:])

@@ -34,6 +34,10 @@ def tile_scatter_matmul_kernel(tc, base, x, w, s, b, offs, out):
         nc.sync.dma_start(gain[:], s.rearrange("(a p) o -> p (a o)", p=P))
         nc.sync.dma_start(shift[:], b.rearrange("(a p) o -> p (a o)", p=P))
 
+        early = held.tile([P, 1], F32, name="early")
+        nc.vector.memset(early[:], 0.0)
+        nc.scalar.activation(early[:], early[:], IDENTITY)
+
         ident = held.tile([P, P], BF16, name="ident")
         make_identity(nc, ident[:])
 

@@ -14,8 +14,8 @@ FLOPS = 2 * K * M * N + 2 * B * M * S
 
 def tile_scatter_matmul_kernel(tc, base, x, w, s, b, offs, out):
     nc = tc.nc
-    base_blocks = base.rearrange("i (a p) t -> i p a t", p=P)
-    out_blocks = out.rearrange("i (a p) t -> i a p t", p=P)
+    base_blocks = base.rearrange("i (p a) t -> i p a t", p=P)
+    out_blocks = out.rearrange("i (p a) t -> i p a t", p=P)
     with (
         tc.tile_pool(name="held", bufs=1) as held,
         tc.psum_pool(name="windows", bufs=1) as windows,
@@ -31,8 +31,8 @@ def tile_scatter_matmul_kernel(tc, base, x, w, s, b, offs, out):
         nc.sync.dma_start(weights[:], w)
         nc.sync.dma_start(moving[:], x)
         nc.sync.dma_start(offsets[:], offs)
-        nc.sync.dma_start(gain[:], s.rearrange("(a p) o -> p (a o)", p=P))
-        nc.sync.dma_start(shift[:], b.rearrange("(a p) o -> p (a o)", p=P))
+        nc.sync.dma_start(gain[:], s.rearrange("(p a) o -> p (a o)", p=P))
+        nc.sync.dma_start(shift[:], b.rearrange("(p a) o -> p (a o)", p=P))
 
         early = held.tile([P, 1], F32, name="early")
         nc.vector.memset(early[:], 0.0)
@@ -52,17 +52,14 @@ def tile_scatter_matmul_kernel(tc, base, x, w, s, b, offs, out):
             piece = offsets[:, i * PIECE_COLS : (i + 1) * PIECE_COLS]
             nc.tensor.matmul(
                 window[i, a][:].indirect(piece),
-                weights[:, a * P : (a + 1) * P],
+                weights[:, a::BLOCKS],
                 moving[:, i * PIECE : (i + 1) * PIECE],
                 start=False,
                 stop=True,
             )
 
-        for i, a in places:
-            result = held.tile([P, S], F32, name=f"result{i}{a}")
-            gain_a, shift_a = gain[:, a : a + 1], shift[:, a : a + 1]
-            if a == 0:
-                nc.scalar.activation(result[:], window[i, a][:], IDENTITY, bias=shift_a, scale=gain_a)
-            else:
-                nc.vector.tensor_scalar(result[:], window[i, a][:], gain_a, shift_a, MULT, ADD)
-            nc.sync.dma_start(out_blocks[i, a], result[:])
+        for i in range(B):
+            result = held.tile([P, BLOCKS, S], F32, name=f"result{i}")
+            nc.scalar.activation(result[:, 0, :], window[i, 0][:], IDENTITY, bias=shift[:, 0:1], scale=gain[:, 0:1])
+            nc.vector.tensor_scalar(result[:, 1, :], window[i, 1][:], gain[:, 1:2], shift[:, 1:2], MULT, ADD)
+            nc.sync.dma_start(out_blocks[i], result[:])

@@ -9,6 +9,8 @@ S, K, M, N, B = 256, 128, 256, 192, 2
 PIECE = N // B
 PIECE_COLS = PIECE // 16
 BLOCKS = M // P
+WARM_COLS = 512
+WARM_UPS = 3
 FLOPS = 2 * K * M * N + 2 * B * M * S
 
 
@@ -38,6 +40,12 @@ def tile_scatter_matmul_kernel(tc, base, x, w, s, b, offs, out):
         nc.vector.memset(early[:], 0.0)
         nc.scalar.activation(early[:], early[:], IDENTITY)
 
+        zeros = held.tile([P, WARM_COLS], BF16, name="zeros")
+        nc.vector.memset(zeros[:], 0.0)
+        spare = windows.tile([P, WARM_COLS], F32, name="spare")
+        for turn in range(WARM_UPS):
+            nc.tensor.matmul(spare[:], zeros[:, :P], zeros[:], start=True, stop=True)
+
         ident = held.tile([P, P], BF16, name="ident")
         make_identity(nc, ident[:])
 
@@ -58,8 +66,11 @@ def tile_scatter_matmul_kernel(tc, base, x, w, s, b, offs, out):
                 stop=True,
             )
 
-        for i in range(B):
-            result = held.tile([P, BLOCKS, S], F32, name=f"result{i}")
-            nc.scalar.activation(result[:, 0, :], window[i, 0][:], IDENTITY, bias=shift[:, 0:1], scale=gain[:, 0:1])
-            nc.vector.tensor_scalar(result[:, 1, :], window[i, 1][:], gain[:, 1:2], shift[:, 1:2], MULT, ADD)
-            nc.sync.dma_start(out_blocks[i], result[:])
+        for i, a in places:
+            result = held.tile([P, S], F32, name=f"result{i}{a}")
+            gain_a, shift_a = gain[:, a : a + 1], shift[:, a : a + 1]
+            if a == 0:
+                nc.scalar.activation(result[:], window[i, a][:], IDENTITY, bias=shift_a, scale=gain_a)
+            else:
+                nc.vector.tensor_scalar(result[:], window[i, a][:], gain_a, shift_a, MULT, ADD)
+            nc.sync.dma_start(out_blocks[i, :, a, :], result[:])

@@ -9,8 +9,7 @@ S, K, M, N, B = 256, 128, 256, 192, 2
 PIECE = N // B
 PIECE_COLS = PIECE // 16
 BLOCKS = M // P
-WARM_COLS = 512
-WARM_UPS = 3
+WARM_UPS = 6
 FLOPS = 2 * K * M * N + 2 * B * M * S
 
 
@@ -40,9 +39,9 @@ def tile_scatter_matmul_kernel(tc, base, x, w, s, b, offs, out):
         nc.vector.memset(early[:], 0.0)
         nc.scalar.activation(early[:], early[:], IDENTITY)
 
-        zeros = held.tile([P, WARM_COLS], BF16, name="zeros")
-        nc.vector.memset(zeros[:], 0.0)
-        spare = windows.tile([P, WARM_COLS], F32, name="spare")
+        zeros = held.tile([P, S], BF16, name="zeros")
+        nc.gpsimd.memset(zeros[:], 0.0)
+        spare = windows.tile([P, S], F32, name="spare")
         for turn in range(WARM_UPS):
             nc.tensor.matmul(spare[:], zeros[:, :P], zeros[:], start=True, stop=True)
 

import concourse.mybir as mybir
from concourse.masks import make_identity

BF16, F32, U16 = mybir.dt.bfloat16, mybir.dt.float32, mybir.dt.uint16
MULT, ADD = mybir.AluOpType.mult, mybir.AluOpType.add
IDENTITY = mybir.ActivationFunctionType.Identity
P = 128
S, K, M, N, B = 256, 128, 256, 192, 2
PIECE = N // B
PIECE_COLS = PIECE // 16
BLOCKS = M // P
WARM_UPS = 6
FLOPS = 2 * K * M * N + 2 * B * M * S


def tile_scatter_matmul_kernel(tc, base, x, w, s, b, offs, out):
    nc = tc.nc
    base_blocks = base.rearrange("i (p a) t -> i p a t", p=P)
    out_blocks = out.rearrange("i (p a) t -> i p a t", p=P)
    with (
        tc.tile_pool(name="held", bufs=1) as held,
        tc.psum_pool(name="windows", bufs=1) as windows,
    ):
        base_tiles = [held.tile([P, BLOCKS, S], BF16, name=f"base{i}") for i in range(B)]
        offsets = held.tile([P, N // 16], U16, name="offsets")
        weights = held.tile([P, M], BF16, name="weights")
        moving = held.tile([P, N], BF16, name="moving")
        gain = held.tile([P, BLOCKS], F32, name="gain")
        shift = held.tile([P, BLOCKS], F32, name="shift")
        for i in range(B):
            nc.sync.dma_start(base_tiles[i][:], base_blocks[i])
        nc.sync.dma_start(weights[:], w)
        nc.sync.dma_start(moving[:], x)
        nc.sync.dma_start(offsets[:], offs)
        nc.sync.dma_start(gain[:], s.rearrange("(p a) o -> p (a o)", p=P))
        nc.sync.dma_start(shift[:], b.rearrange("(p a) o -> p (a o)", p=P))

        early = held.tile([P, 1], F32, name="early")
        nc.vector.memset(early[:], 0.0)
        nc.scalar.activation(early[:], early[:], IDENTITY)

        zeros = held.tile([P, S], BF16, name="zeros")
        nc.gpsimd.memset(zeros[:], 0.0)
        spare = windows.tile([P, S], F32, name="spare")
        for turn in range(WARM_UPS):
            nc.tensor.matmul(spare[:], zeros[:, :P], zeros[:], start=True, stop=True)

        ident = held.tile([P, P], BF16, name="ident")
        make_identity(nc, ident[:])

        places = [(i, a) for i in range(B) for a in range(BLOCKS)]
        window = {
            (i, a): windows.tile([P, S], F32, name=f"window{i}{a}") for i, a in places
        }
        for i, a in places:
            nc.tensor.matmul(window[i, a][:], ident[:], base_tiles[i][:, a, :], start=True, stop=False)

        for i, a in places:
            piece = offsets[:, i * PIECE_COLS : (i + 1) * PIECE_COLS]
            nc.tensor.matmul(
                window[i, a][:].indirect(piece),
                weights[:, a::BLOCKS],
                moving[:, i * PIECE : (i + 1) * PIECE],
                start=False,
                stop=True,
            )

        for i, a in places:
            result = held.tile([P, S], F32, name=f"result{i}{a}")
            gain_a, shift_a = gain[:, a : a + 1], shift[:, a : a + 1]
            if a == 0:
                nc.scalar.activation(result[:], window[i, a][:], IDENTITY, bias=shift_a, scale=gain_a)
            else:
                nc.vector.tensor_scalar(result[:], window[i, a][:], gain_a, shift_a, MULT, ADD)
            nc.sync.dma_start(out_blocks[i, :, a, :], result[:])
